import numpy as np, ml_dtypes
CORES = [97,101,225,229,353,357,481,485]
N = 8
S, B = 2, 256
NT = N * S
def setup_inputs(rng):
    a = (rng.standard_normal((128, 128), dtype=np.float32) / 12).astype(ml_dtypes.bfloat16)
    return {"x": rng.standard_normal((N, 128, S * B), dtype=np.float32).astype(ml_dtypes.bfloat16), "a": np.broadcast_to(a, (N, 128, 128)).copy(), "at": np.broadcast_to(a.T, (N, 128, 128)).copy()}
def setup_inputs_big(rng):
    d = setup_inputs(rng)
    for k in ("x",): d[k] = (d[k].astype(np.float32) * 1048576.0).astype(d[k].dtype)
    return d
def setup_inputs_small(rng):
    d = setup_inputs(rng)
    for k in ("x",): d[k] = (d[k].astype(np.float32) * (1 / 1048576.0)).astype(d[k].dtype)
    return d
def setup_inputs_apart(rng):
    d = setup_inputs(rng)
    f = (10.0 ** rng.permutation(np.linspace(-1.5, 1.5, N))).astype(np.float32).reshape(N, 1, 1)
    for k in ("x",): d[k] = (d[k].astype(np.float32) * f).astype(d[k].dtype)
    return d
def reference(x, a, at):
    A = a[0].astype(np.float64); X = [x[t // S][:, B * (t % S):B * (t % S) + B].astype(np.float64) for t in range(NT)]
    f = [None] * NT; b = [None] * NT; h = np.zeros((128, B))
    for t in range(NT):
        h = A.T @ h + X[t]; f[t] = h
    h = np.zeros((128, B))
    for t in range(NT - 1, -1, -1):
        h = A.T @ h + X[t]; b[t] = h
    return {"y": np.stack([np.concatenate([f[r * S + s] + b[r * S + s] for s in range(S)], axis=1) for r in range(N)]).astype(ml_dtypes.bfloat16)}

@@ -1,0 +1,247 @@
+from concourse.bass import DstId, RemoteDMATransfer
+from concourse.mybir import AluOpType
+
+B = 256
+M = 128
+
+A1, A2, AT2, A3, A4, AT4, S6, S7, S8 = range(9)
+
+SCRATCH = {
+    "xs": ("sbuf", [M, 2 * B], "bfloat16"),
+    "w": ("sbuf", [M, 9 * M], "bfloat16"),
+    "at1": ("sbuf", [M, M], "bfloat16"),
+    "cd": ("sbuf", [M, 2 * B], "bfloat16"),
+    "loc": ("sbuf", [M, 2 * B], "float32"),
+    "rel": ("sbuf", [M, B], "bfloat16"),
+    "in1": ("sbuf", [M, 3 * B], "bfloat16"),
+    "in2": ("sbuf", [M, 2 * B], "bfloat16"),
+    "yo": ("sbuf", [M, 2 * B], "bfloat16"),
+    "pf": ("psum", [M, 512], "float32"),
+    "pb": ("psum", [M, 512], "float32"),
+    "pp": ("psum", [M, 512], "float32"),
+    "pr": ("psum", [M, 512], "float32"),
+    "py0": ("psum", [M, 512], "float32"),
+    "py1": ("psum", [M, 512], "float32"),
+}
+NLOCAL = 28
+SEMAPHORES = ["h1A", "h1B", "h1C", "h2A", "h2B", "sent"] + ["q%d" % i for i in range(NLOCAL)]
+
+SEND1 = {0: [[("f", 3, "A"), ("f", 1, "A")]],
+         1: [[("f", 3, "B"), ("f", 0, "A")], [("b", 0, "B")]],
+         2: [[("f", 5, "C"), ("f", 3, "C")]],
+         3: [[("f", 5, "B"), ("b", 2, "A")]]}
+SEND2 = {0: [(6, "B")], 1: [(7, "B"), (2, "B")], 2: [(0, "A"), (1, "A")], 3: [(4, "A"), (5, "A")]}
+FROM1 = {0: {"A": 1, "B": 1}, 1: {"A": 0}, 2: {"A": 3, "B": 4, "C": 5}, 3: {"A": 0, "B": 1, "C": 2}}
+FROM2 = {0: {"A": 2, "B": 6}, 1: {"A": 2, "B": 7}, 2: {"A": 4, "B": 1}, 3: {"A": 4}}
+REL = {0: ("A", [("f", 2)]), 1: ("f", [("A", 2)]),
+       2: ("b", [("C", 6), ("A", 2), ("B", 4)]), 3: ("f", [("C", 2), ("A", 6), ("B", 4)])}
+FIN = {0: [(1, "B", 2, 1), (2, "B", 12, 11), (2, "A", 4, 3)],
+       1: [(1, "A", 1, 2), (2, "B", 10, 9), (2, "A", 2, 1)],
+       2: [(1, "A", 2, 1), (2, "B", 1, 2), (2, "A", 4, 3)],
+       3: [(1, "C", 1, 2), (1, "B", 3, 4), (1, "A", 5, 6), (2, "A", 2, 1)]}
+COL = {"A": 0, "B": 1, "C": 2}
+
+
+def _bits(mask):
+    return [e for e in range(mask.bit_length()) if (mask >> e) & 1]
+
+
+def _pack(engines):
+    return sum(1 << e for e in engines)
+
+
+def rank_program(g, core, T, topo):
+    rank = T.rank_of(core)
+    if rank is None:
+        return
+    n = len(T.cores)
+    mirrored = rank >= n // 2
+    rho = n - 1 - rank if mirrored else rank
+
+    def peer(k):
+        return T.cores[n - 1 - k if mirrored else k]
+
+    def same_chip(p, q):
+        return topo.host(p) == topo.host(q) and topo.chip(p) == topo.chip(q)
+
+    def engines(src, dst):
+        if not same_chip(src, dst):
+            return _bits(topo.mask(src, dst))
+        away = 0
+        for c in T.cores:
+            if not same_chip(src, c) and topo.may_write(src, c):
+                away |= topo.mask(src, c)
+        return [e for e in _bits(topo.mask(src, dst)) if not (away >> e) & 1]
+
+    te, ve, sy, sc = g.tensor, g.vector, g.sync, g.scalar
+    pool = [0]
+
+    def sem():
+        pool[0] += 1
+        return T.sem["q%d" % (pool[0] - 1)]
+
+    def blk(t, j, width=B):
+        return t[:, j * width:(j + 1) * width]
+
+    def W(j, k=1):
+        return T.w[:, j * M:(j + k) * M]
+
+    b0, b1 = (1, 0) if mirrored else (0, 1)
+    X0, X1 = blk(T.xs, b0), blk(T.xs, b1)
+    FWD, BWD = blk(T.cd, 0), blk(T.cd, 1)
+    end_host = rho < 2
+    slot = {1: A1, 2: A2, 3: A3, 4: A4}
+    if end_host:
+        low = {0: 3, 1: 1}[rho]
+        hi = slot[low]
+        slot.update({8 + low: S7, 9 + low: S8})
+    else:
+        slot.update({5: S6, 6: S7})
+
+    ld_x, ld_a, ld_at = sem(), sem(), sem()
+    sy.dma_start(T.xs[:], T.x[:]).then_inc(ld_x, 16)
+    sc.dma_start(W(A1), T.a[:]).then_inc(ld_a, 16)
+    sc.dma_start(T.at1[:], T.at[:]).then_inc(ld_at, 16)
+
+    m_f, m_b, v_f, v_b = sem(), sem(), sem(), sem()
+    te.wait_ge(ld_a, 16)
+    te.wait_ge(ld_x, 16)
+    te.matmul(T.pf[:, 0:B], W(A1), X0, True, True).then_inc(m_f, 1)
+    te.matmul(T.pb[:, 0:B], W(A1), X1, True, True).then_inc(m_b, 1)
+    ve.wait_ge(ld_x, 16)
+
+    def carry_f():
+        ve.wait_ge(m_f, 1)
+        ve.tensor_tensor(FWD, T.pf[:, 0:B], X1, AluOpType.add).then_inc(v_f, 1)
+
+    def carry_b():
+        ve.wait_ge(m_b, 1)
+        ve.tensor_tensor(BWD, T.pb[:, 0:B], X0, AluOpType.add).then_inc(v_b, 1)
+
+    def step(first, products, after):
+        ms, vs = sem(), sem()
+        for s, c in after:
+            te.wait_ge(s, c)
+        at = 0
+        for lhsT, rhs, k in products:
+            te.matmul(T.pp[:, at * M:(at + k) * M], lhsT, rhs, True, True).then_inc(ms, 1)
+            at += k
+        return (ms, len(products), first, at, vs)
+
+    def step_out(st):
+        ms, cnt, first, k, vs = st
+        ve.wait_ge(ms, cnt)
+        ve.tensor_copy(W(first, k), T.pp[:, 0:k * M]).then_inc(vs, 1)
+        return vs
+
+    plain, terms = REL[rho]
+    m_r, v_r = sem(), sem()
+
+    def src_of(k):
+        if k == "f":
+            return FWD
+        if k == "b":
+            return BWD
+        return blk(T.in1, COL[k])
+
+    def ready(q, k):
+        if k == "f":
+            q.wait_ge(v_f, 1)
+        elif k == "b":
+            q.wait_ge(v_b, 1)
+        else:
+            q.wait_ge(T.sem["h1" + k], len(engines(peer(FROM1[rho][k]), core)))
+
+    def relay_mm():
+        for i, (k, p) in enumerate(terms):
+            ready(te, k)
+            te.matmul(T.pr[:, 0:B], W(slot[p]), src_of(k), i == 0, i == len(terms) - 1).then_inc(m_r, 1)
+
+    def relay_out():
+        ready(ve, plain)
+        ve.wait_ge(m_r, len(terms))
+        ve.tensor_tensor(T.rel[:], T.pr[:, 0:B], src_of(plain), AluOpType.add).then_inc(v_r, 1)
+
+    carry_f()
+    if not end_host:
+        carry_b()
+    s1 = step(A2, [(T.at1[:], W(A1), 1), (W(A1), T.at1[:], 1)], [(ld_at, 16)])
+    c1 = step_out(s1)
+    if end_host:
+        carry_b()
+    if rho == 0:
+        te.wait_ge(c1, 1)
+        relay_mm()
+    s2 = step(A3, [(W(AT2), W(A1, 2), 2), (W(A2), W(AT2), 1)], [(c1, 1)])
+    c2 = step_out(s2)
+    if end_host:
+        if rho == 1:
+            relay_mm()
+        relay_out()
+        s3 = step(S6, [(W(A4), W(AT4), 1)], [(c2, 1)])
+        c3 = step_out(s3)
+        s4 = step(S7, [(W(S6), W(hi, 2), 2)], [(c3, 1)])
+        c_last = step_out(s4)
+    else:
+        s3 = step(S6, [(W(AT4), W(A1, 2), 2)], [(c2, 1)])
+        c_last = step_out(s3)
+        te.wait_ge(c_last, 1)
+        relay_mm()
+        relay_out()
+    te.wait_ge(c_last, 1)
+
+    v_l = sem()
+    ve.wait_ge(v_f, 1)
+    ve.wait_ge(v_b, 1)
+    ve.tensor_tensor(blk(T.loc, 0), X0, BWD, AluOpType.add).then_inc(v_l, 1)
+    ve.tensor_tensor(blk(T.loc, 1), FWD, X1, AluOpType.add).then_inc(v_l, 1)
+
+    m_y0, m_y1 = sem(), sem()
+    fin = FIN[rho]
+    for i, (rnd, k, p0, p1) in enumerate(fin):
+        frm = (FROM1 if rnd == 1 else FROM2)[rho][k]
+        te.wait_ge(T.sem["h%d%s" % (rnd, k)], len(engines(peer(frm), core)))
+        src = blk(T.in1 if rnd == 1 else T.in2, COL[k])
+        te.matmul(T.py0[:, 0:B], W(slot[p0]), src, i == 0, i == len(fin) - 1).then_inc(m_y0, 1)
+        te.matmul(T.py1[:, 0:B], W(slot[p1]), src, i == 0, i == len(fin) - 1).then_inc(m_y1, 1)
+
+    v_y0, v_y1, st0, st1 = sem(), sem(), sem(), sem()
+    ve.wait_ge(v_l, 2)
+    ve.wait_ge(m_y0, len(fin))
+    ve.tensor_tensor(blk(T.yo, b0), T.py0[:, 0:B], blk(T.loc, 0), AluOpType.add).then_inc(v_y0, 1)
+    ve.wait_ge(m_y1, len(fin))
+    ve.tensor_tensor(blk(T.yo, b1), T.py1[:, 0:B], blk(T.loc, 1), AluOpType.add).then_inc(v_y1, 1)
+    sy.wait_ge(v_y0, 1)
+    sy.dma_start(blk(T.y, b0), blk(T.yo, b0)).then_inc(st0, 16)
+    sy.wait_ge(st0, 16)
+    sc.wait_ge(v_y1, 1)
+    sc.dma_start(blk(T.y, b1), blk(T.yo, b1)).then_inc(st1, 16)
+    sc.wait_ge(st1, 16)
+
+    sent = 0
+
+    def dst_id(d):
+        rid, pid = topo.addr(d, core)
+        return DstId(rid=rid, pnc=pid)
+
+    for call in SEND1[rho]:
+        for k in sorted(set(k for k, _, _ in call)):
+            ready(g, k)
+        trs = []
+        for k, to, b in call:
+            d = peer(to)
+            es = engines(core, d)
+            sent += len(es)
+            trs.append(RemoteDMATransfer(dst_ids=[dst_id(d)], dma_engine_mask=_pack(es), remote_sem=T.sem["h1" + b],
+                                         src=src_of(k), dst=blk(T.in1, COL[b])))
+        g.remote_dma_fused(trs, local_sem=T.sem.sent)
+
+    g.wait_ge(v_r, 1)
+    ds = [peer(to) for to, _ in SEND2[rho]]
+    b = SEND2[rho][0][1]
+    es = engines(core, ds[0])
+    sent += len(es)
+    g.remote_dma_fused([RemoteDMATransfer(dst_ids=[dst_id(d) for d in ds], dma_engine_mask=_pack(es),
+                                          remote_sem=T.sem["h2" + b], srcs=[T.rel[:]],
+                                          dsts=[blk(T.in2, COL[b]) for d in ds])], local_sem=T.sem.sent)
+    g.wait_ge(T.sem.sent, sent)

@@ -13,7 +13,8 @@ SCRATCH = {
     "cd": ("sbuf", [M, 2 * B], "bfloat16"),
     "loc": ("sbuf", [M, 2 * B], "float32"),
     "rel": ("sbuf", [M, B], "bfloat16"),
-    "in1": ("sbuf", [M, 3 * B], "bfloat16"),
+    "px": ("sbuf", [M, 2 * B], "bfloat16"),
+    "in1": ("sbuf", [M, 2 * B], "bfloat16"),
     "in2": ("sbuf", [M, 2 * B], "bfloat16"),
     "yo": ("sbuf", [M, 2 * B], "bfloat16"),
     "pf": ("psum", [M, 512], "float32"),
@@ -24,22 +25,19 @@ SCRATCH = {
     "py1": ("psum", [M, 512], "float32"),
 }
 NLOCAL = 28
-SEMAPHORES = ["h1A", "h1B", "h1C", "h2A", "h2B", "sent"] + ["q%d" % i for i in range(NLOCAL)]
+SEMAPHORES = ["hp", "h1A", "h1B", "h2A", "h2B", "sent"] + ["q%d" % i for i in range(NLOCAL)]
 
-SEND1 = {0: [[("f", 3, "A"), ("f", 1, "A")]],
-         1: [[("f", 3, "B"), ("f", 0, "A")], [("b", 0, "B")]],
-         2: [[("f", 5, "C"), ("f", 3, "C")]],
-         3: [[("f", 5, "B"), ("b", 2, "A")]]}
+SEND1 = {0: ("f", 3, "A"), 1: ("f", 3, "B"), 2: ("f", 5, "A"), 3: ("f", 5, "B")}
 SEND2 = {0: [(6, "B")], 1: [(7, "B"), (2, "B")], 2: [(0, "A"), (1, "A")], 3: [(4, "A"), (5, "A")]}
-FROM1 = {0: {"A": 1, "B": 1}, 1: {"A": 0}, 2: {"A": 3, "B": 4, "C": 5}, 3: {"A": 0, "B": 1, "C": 2}}
+FROM1 = {0: {}, 1: {}, 2: {"A": 5, "B": 4}, 3: {"A": 0, "B": 1}}
 FROM2 = {0: {"A": 2, "B": 6}, 1: {"A": 2, "B": 7}, 2: {"A": 4, "B": 1}, 3: {"A": 4}}
-REL = {0: ("A", [("f", 2)]), 1: ("f", [("A", 2)]),
-       2: ("b", [("C", 6), ("A", 2), ("B", 4)]), 3: ("f", [("C", 2), ("A", 6), ("B", 4)])}
-FIN = {0: [(1, "B", 2, 1), (2, "B", 12, 11), (2, "A", 4, 3)],
-       1: [(1, "A", 1, 2), (2, "B", 10, 9), (2, "A", 2, 1)],
-       2: [(1, "A", 2, 1), (2, "B", 1, 2), (2, "A", 4, 3)],
-       3: [(1, "C", 1, 2), (1, "B", 3, 4), (1, "A", 5, 6), (2, "A", 2, 1)]}
-COL = {"A": 0, "B": 1, "C": 2}
+REL = {0: ("P1", [("f", 2), ("P0", 1)]), 1: ("f", [("P0", 3), ("P1", 2)]),
+       2: ("b", [("P1", 3), ("P0", 2), ("A", 6), ("B", 4)]), 3: ("f", [("P0", 3), ("P1", 2), ("A", 6), ("B", 4)])}
+FIN = {0: [(1, "P1", 3, 2), (1, "P0", 2, 1), (2, "B", 12, 11), (2, "A", 4, 3)],
+       1: [(1, "P0", 2, 3), (1, "P1", 1, 2), (2, "B", 10, 9), (2, "A", 2, 1)],
+       2: [(1, "P1", 3, 2), (1, "P0", 2, 1), (2, "B", 1, 2), (2, "A", 4, 3)],
+       3: [(1, "P0", 2, 3), (1, "P1", 1, 2), (1, "B", 3, 4), (1, "A", 5, 6), (2, "A", 2, 1)]}
+COL = {"A": 0, "B": 1}
 
 
 def _bits(mask):
@@ -89,6 +87,8 @@ def rank_program(g, core, T, topo):
     b0, b1 = (1, 0) if mirrored else (0, 1)
     X0, X1 = blk(T.xs, b0), blk(T.xs, b1)
     FWD, BWD = blk(T.cd, 0), blk(T.cd, 1)
+    fellow = [c for c in T.cores if c != core and same_chip(c, core)][0]
+    own = {"f": FWD, "b": BWD, "P0": blk(T.px, b0), "P1": blk(T.px, b1)}
     end_host = rho < 2
     slot = {1: A1, 2: A2, 3: A3, 4: A4}
     if end_host:
@@ -138,17 +138,15 @@ def rank_program(g, core, T, topo):
     m_r, v_r = sem(), sem()
 
     def src_of(k):
-        if k == "f":
-            return FWD
-        if k == "b":
-            return BWD
-        return blk(T.in1, COL[k])
+        return own[k] if k in own else blk(T.in1, COL[k])
 
     def ready(q, k):
         if k == "f":
             q.wait_ge(v_f, 1)
         elif k == "b":
             q.wait_ge(v_b, 1)
+        elif k in own:
+            q.wait_ge(T.sem.hp, len(engines(fellow, core)))
         else:
             q.wait_ge(T.sem["h1" + k], len(engines(peer(FROM1[rho][k]), core)))
 
@@ -163,20 +161,14 @@ def rank_program(g, core, T, topo):
         ve.tensor_tensor(T.rel[:], T.pr[:, 0:B], src_of(plain), AluOpType.add).then_inc(v_r, 1)
 
     carry_f()
-    if not end_host:
-        carry_b()
     s1 = step(A2, [(T.at1[:], W(A1), 1), (W(A1), T.at1[:], 1)], [(ld_at, 16)])
     c1 = step_out(s1)
-    if end_host:
-        carry_b()
-    if rho == 0:
-        te.wait_ge(c1, 1)
-        relay_mm()
+    carry_b()
     s2 = step(A3, [(W(AT2), W(A1, 2), 2), (W(A2), W(AT2), 1)], [(c1, 1)])
     c2 = step_out(s2)
     if end_host:
-        if rho == 1:
-            relay_mm()
+        te.wait_ge(c2, 1)
+        relay_mm()
         relay_out()
         s3 = step(S6, [(W(A4), W(AT4), 1)], [(c2, 1)])
         c3 = step_out(s3)
@@ -199,9 +191,12 @@ def rank_program(g, core, T, topo):
     m_y0, m_y1 = sem(), sem()
     fin = FIN[rho]
     for i, (rnd, k, p0, p1) in enumerate(fin):
-        frm = (FROM1 if rnd == 1 else FROM2)[rho][k]
-        te.wait_ge(T.sem["h%d%s" % (rnd, k)], len(engines(peer(frm), core)))
-        src = blk(T.in1 if rnd == 1 else T.in2, COL[k])
+        if rnd == 1:
+            ready(te, k)
+            src = src_of(k)
+        else:
+            te.wait_ge(T.sem["h2" + k], len(engines(peer(FROM2[rho][k]), core)))
+            src = blk(T.in2, COL[k])
         te.matmul(T.py0[:, 0:B], W(slot[p0]), src, i == 0, i == len(fin) - 1).then_inc(m_y0, 1)
         te.matmul(T.py1[:, 0:B], W(slot[p1]), src, i == 0, i == len(fin) - 1).then_inc(m_y1, 1)
 
@@ -224,17 +219,18 @@ def rank_program(g, core, T, topo):
         rid, pid = topo.addr(d, core)
         return DstId(rid=rid, pnc=pid)
 
-    for call in SEND1[rho]:
-        for k in sorted(set(k for k, _, _ in call)):
-            ready(g, k)
-        trs = []
-        for k, to, b in call:
-            d = peer(to)
-            es = engines(core, d)
-            sent += len(es)
-            trs.append(RemoteDMATransfer(dst_ids=[dst_id(d)], dma_engine_mask=_pack(es), remote_sem=T.sem["h1" + b],
-                                         src=src_of(k), dst=blk(T.in1, COL[b])))
-        g.remote_dma_fused(trs, local_sem=T.sem.sent)
+    def write(src, dst, d, remote_sem):
+        rid, pid = topo.addr(d, core)
+        es = engines(core, d)
+        g.remote_dma(out_ap=dst, in_ap=src, remote_sem=remote_sem, local_sem=T.sem.sent, pid=pid, routing_id=rid,
+                     dma_engine_mask=_pack(es))
+        return len(es)
+
+    g.wait_ge(ld_x, 16)
+    sent += write(T.xs[:], T.px[:], fellow, T.sem.hp)
+    k, to, b = SEND1[rho]
+    ready(g, k)
+    sent += write(src_of(k), blk(T.in1, COL[b]), peer(to), T.sem["h1" + b])
 
     g.wait_ge(v_r, 1)
     ds = [peer(to) for to, _ in SEND2[rho]]

@@ -3,6 +3,7 @@ from concourse.mybir import AluOpType
 
 B = 256
 M = 128
+H = B // 2
 
 A1, A2, AT2, A3, A4, AT4, S6, S7, S8 = range(9)
 
@@ -14,30 +15,30 @@ SCRATCH = {
     "loc": ("sbuf", [M, 2 * B], "float32"),
     "rel": ("sbuf", [M, B], "bfloat16"),
     "px": ("sbuf", [M, 2 * B], "bfloat16"),
-    "in1": ("sbuf", [M, 2 * B], "bfloat16"),
+    "in1": ("sbuf", [M, 4 * H], "bfloat16"),
     "in2": ("sbuf", [M, 2 * B], "bfloat16"),
     "yo": ("sbuf", [M, 2 * B], "bfloat16"),
     "pf": ("psum", [M, 512], "float32"),
     "pb": ("psum", [M, 512], "float32"),
     "pp": ("psum", [M, 512], "float32"),
     "pr": ("psum", [M, 512], "float32"),
+    "ps": ("psum", [M, 512], "float32"),
     "py0": ("psum", [M, 512], "float32"),
     "py1": ("psum", [M, 512], "float32"),
 }
-NLOCAL = 28
-SEMAPHORES = ["hp", "h1A", "h1B", "h2A", "h2B", "sent"] + ["q%d" % i for i in range(NLOCAL)]
+NLOCAL = 32
+SEMAPHORES = (["hp", "h2A0", "h2A1", "h2B", "sent"] + ["h1_%d" % i for i in range(4)] + ["q%d" % i for i in range(NLOCAL)])
 
-SEND1 = {0: ("f", 3, "A"), 1: ("f", 3, "B"), 2: ("f", 5, "A"), 3: ("f", 5, "B")}
-SEND2 = {0: [(6, "B")], 1: [(7, "B"), (2, "B")], 2: [(0, "A"), (1, "A")], 3: [(4, "A"), (5, "A")]}
-FROM1 = {0: {}, 1: {}, 2: {"A": 5, "B": 4}, 3: {"A": 0, "B": 1}}
-FROM2 = {0: {"A": 2, "B": 6}, 1: {"A": 2, "B": 7}, 2: {"A": 4, "B": 1}, 3: {"A": 4}}
-REL = {0: ("P1", [("f", 2), ("P0", 1)]), 1: ("f", [("P0", 3), ("P1", 2)]),
-       2: ("b", [("P1", 3), ("P0", 2), ("A", 6), ("B", 4)]), 3: ("f", [("P0", 3), ("P1", 2), ("A", 6), ("B", 4)])}
-FIN = {0: [(1, "P1", 3, 2), (1, "P0", 2, 1), (2, "B", 12, 11), (2, "A", 4, 3)],
-       1: [(1, "P0", 2, 3), (1, "P1", 1, 2), (2, "B", 10, 9), (2, "A", 2, 1)],
-       2: [(1, "P1", 3, 2), (1, "P0", 2, 1), (2, "B", 1, 2), (2, "A", 4, 3)],
-       3: [(1, "P0", 2, 3), (1, "P1", 1, 2), (1, "B", 3, 4), (1, "A", 5, 6), (2, "A", 2, 1)]}
-COL = {"A": 0, "B": 1}
+SEND1 = {0: ((2, 3), 0), 1: ((2, 3), 1), 2: ((4, 5), 3), 3: ((4, 5), 2)}
+RSLOT = {"R0": 0, "R1": 1, "R4": 2, "R5": 3}
+SENDB = {0: (6, 3), 1: (7, 2)}
+REL = {0: ("P1", [("f", 2), ("P0", 1)]), 1: ("f", [("P0", 3), ("P1", 2)])}
+RELF = {2: ("P1", [("f", 2), ("P0", 1), ("R0", 6), ("R1", 4)]), 3: ("f", [("P0", 3), ("P1", 2), ("R0", 6), ("R1", 4)])}
+RELS = {2: ("b", [("P1", 3), ("P0", 2), ("R5", 6), ("R4", 4)]), 3: ("P0", [("b", 2), ("P1", 1), ("R5", 6), ("R4", 4)])}
+FIN = {0: [("P1", 3, 2), ("P0", 2, 1), ("B", 12, 11), ("A", 4, 3)],
+       1: [("P0", 2, 3), ("P1", 1, 2), ("B", 10, 9), ("A", 2, 1)],
+       2: [("P1", 3, 2), ("P0", 2, 1), ("B", 1, 2), ("A", 4, 3)],
+       3: [("P0", 2, 3), ("P1", 1, 2), ("B", 3, 4), ("A", 2, 1)]}
 
 
 def _bits(mask):
@@ -71,6 +72,9 @@ def rank_program(g, core, T, topo):
                 away |= topo.mask(src, c)
         return [e for e in _bits(topo.mask(src, dst)) if not (away >> e) & 1]
 
+    def half_of(c):
+        return T.rank_of(c) % 2
+
     te, ve, sy, sc = g.tensor, g.vector, g.sync, g.scalar
     pool = [0]
 
@@ -88,8 +92,9 @@ def rank_program(g, core, T, topo):
     X0, X1 = blk(T.xs, b0), blk(T.xs, b1)
     FWD, BWD = blk(T.cd, 0), blk(T.cd, 1)
     fellow = [c for c in T.cores if c != core and same_chip(c, core)][0]
-    own = {"f": FWD, "b": BWD, "P0": blk(T.px, b0), "P1": blk(T.px, b1)}
+    own = {"f": (T.cd, 0), "b": (T.cd, 1), "P0": (T.px, b0), "P1": (T.px, b1)}
     end_host = rho < 2
+    my_half = half_of(core)
     slot = {1: A1, 2: A2, 3: A3, 4: A4}
     if end_host:
         low = {0: 3, 1: 1}[rho]
@@ -134,11 +139,11 @@ def rank_program(g, core, T, topo):
         ve.tensor_copy(W(first, k), T.pp[:, 0:k * M]).then_inc(vs, 1)
         return vs
 
-    plain, terms = REL[rho]
-    m_r, v_r = sem(), sem()
-
-    def src_of(k):
-        return own[k] if k in own else blk(T.in1, COL[k])
+    def src_of(k, half=None):
+        if k in RSLOT:
+            return blk(T.in1, RSLOT[k], H)
+        t, j = own[k]
+        return blk(t, j) if half is None else blk(t, 2 * j + half, H)
 
     def ready(q, k):
         if k == "f":
@@ -148,17 +153,34 @@ def rank_program(g, core, T, topo):
         elif k in own:
             q.wait_ge(T.sem.hp, len(engines(fellow, core)))
         else:
-            q.wait_ge(T.sem["h1" + k], len(engines(peer(FROM1[rho][k]), core)))
+            q.wait_ge(T.sem["h1_%d" % RSLOT[k]], n_half)
+
+    n_away = len([e for c in T.cores if not same_chip(core, c) and topo.may_write(core, c)
+                  for e in engines(core, c)][:len(engines(core, [c for c in T.cores if not same_chip(core, c)
+                                                                  and topo.may_write(core, c)][0]))])
+    n_half = n_away // 2
+
+    v_r = sem()
+    if end_host:
+        sums = [(REL[rho], T.pr, None, T.rel[:], sem())]
+    else:
+        sums = [(RELF[rho], T.pr, my_half, blk(T.rel, 0, H), sem()), (RELS[rho], T.ps, my_half, blk(T.rel, 1, H), sem())]
 
     def relay_mm():
-        for i, (k, p) in enumerate(terms):
-            ready(te, k)
-            te.matmul(T.pr[:, 0:B], W(slot[p]), src_of(k), i == 0, i == len(terms) - 1).then_inc(m_r, 1)
+        depth = len(sums[0][0][1])
+        for i in range(depth):
+            for (plain, terms), bank, half, out, ms in sums:
+                k, p = terms[i]
+                ready(te, k)
+                width = B if half is None else H
+                te.matmul(bank[:, 0:width], W(slot[p]), src_of(k, half), i == 0, i == depth - 1).then_inc(ms, 1)
 
     def relay_out():
-        ready(ve, plain)
-        ve.wait_ge(m_r, len(terms))
-        ve.tensor_tensor(T.rel[:], T.pr[:, 0:B], src_of(plain), AluOpType.add).then_inc(v_r, 1)
+        for (plain, terms), bank, half, out, ms in sums:
+            ready(ve, plain)
+            ve.wait_ge(ms, len(terms))
+            width = B if half is None else H
+            ve.tensor_tensor(out, bank[:, 0:width], src_of(plain, half), AluOpType.add).then_inc(v_r, 1)
 
     carry_f()
     s1 = step(A2, [(T.at1[:], W(A1), 1), (W(A1), T.at1[:], 1)], [(ld_at, 16)])
@@ -190,13 +212,17 @@ def rank_program(g, core, T, topo):
 
     m_y0, m_y1 = sem(), sem()
     fin = FIN[rho]
-    for i, (rnd, k, p0, p1) in enumerate(fin):
-        if rnd == 1:
+    for i, (k, p0, p1) in enumerate(fin):
+        if k == "A":
+            te.wait_ge(T.sem.h2A0, n_half)
+            te.wait_ge(T.sem.h2A1, n_half)
+            src = blk(T.in2, 0)
+        elif k == "B":
+            te.wait_ge(T.sem.h2B, n_away)
+            src = blk(T.in2, 1)
+        else:
             ready(te, k)
             src = src_of(k)
-        else:
-            te.wait_ge(T.sem["h2" + k], len(engines(peer(FROM2[rho][k]), core)))
-            src = blk(T.in2, COL[k])
         te.matmul(T.py0[:, 0:B], W(slot[p0]), src, i == 0, i == len(fin) - 1).then_inc(m_y0, 1)
         te.matmul(T.py1[:, 0:B], W(slot[p1]), src, i == 0, i == len(fin) - 1).then_inc(m_y1, 1)
 
@@ -219,25 +245,38 @@ def rank_program(g, core, T, topo):
         rid, pid = topo.addr(d, core)
         return DstId(rid=rid, pnc=pid)
 
-    def write(src, dst, d, remote_sem):
-        rid, pid = topo.addr(d, core)
-        es = engines(core, d)
-        g.remote_dma(out_ap=dst, in_ap=src, remote_sem=remote_sem, local_sem=T.sem.sent, pid=pid, routing_id=rid,
-                     dma_engine_mask=_pack(es))
-        return len(es)
+    def transfer(src, dst, ds, es, remote_sem):
+        return RemoteDMATransfer(dst_ids=[dst_id(d) for d in ds], dma_engine_mask=_pack(es), remote_sem=remote_sem,
+                                 srcs=[src], dsts=[dst for d in ds])
 
     g.wait_ge(ld_x, 16)
-    sent += write(T.xs[:], T.px[:], fellow, T.sem.hp)
-    k, to, b = SEND1[rho]
-    ready(g, k)
-    sent += write(src_of(k), blk(T.in1, COL[b]), peer(to), T.sem["h1" + b])
-
-    g.wait_ge(v_r, 1)
-    ds = [peer(to) for to, _ in SEND2[rho]]
-    b = SEND2[rho][0][1]
-    es = engines(core, ds[0])
+    rid, pid = topo.addr(fellow, core)
+    es = engines(core, fellow)
+    g.remote_dma(out_ap=T.px[:], in_ap=T.xs[:], remote_sem=T.sem.hp, local_sem=T.sem.sent, pid=pid, routing_id=rid,
+                 dma_engine_mask=_pack(es))
     sent += len(es)
-    g.remote_dma_fused([RemoteDMATransfer(dst_ids=[dst_id(d) for d in ds], dma_engine_mask=_pack(es),
-                                          remote_sem=T.sem["h2" + b], srcs=[T.rel[:]],
-                                          dsts=[blk(T.in2, COL[b]) for d in ds])], local_sem=T.sem.sent)
+    relays, land = SEND1[rho]
+    g.wait_ge(v_f, 1)
+    trs = []
+    for j, k in enumerate(relays):
+        d = peer(k)
+        es = engines(core, d)[j::2]
+        trs.append(transfer(blk(T.cd, half_of(d), H), blk(T.in1, land, H), [d], es, T.sem["h1_%d" % land]))
+        sent += len(es)
+    g.remote_dma_fused(trs, local_sem=T.sem.sent)
+
+    g.wait_ge(v_r, len(sums))
+    if end_host:
+        ds = [peer(k) for k in SENDB[rho]]
+        es = engines(core, ds[0])
+        trs = [transfer(T.rel[:], blk(T.in2, 1), ds, es, T.sem.h2B)]
+        sent += len(es)
+    else:
+        trs = []
+        for j, ks in enumerate(((4, 5), (0, 1))):
+            ds = [peer(k) for k in ks]
+            es = engines(core, ds[0])[j::2]
+            trs.append(transfer(blk(T.rel, j, H), blk(T.in2, my_half, H), ds, es, T.sem["h2A%d" % my_half]))
+            sent += len(es)
+    g.remote_dma_fused(trs, local_sem=T.sem.sent)
     g.wait_ge(T.sem.sent, sent)

@@ -5,17 +5,18 @@ B = 256
 M = 128
 H = B // 2
 
-A1, A2, AT2, A3, A4, AT4, S6, S7, S8 = range(9)
+A1, A2, AT2, A3, A4, AT4, A5, A6, A7, A8 = range(10)
 
 SCRATCH = {
     "xs": ("sbuf", [M, 2 * B], "bfloat16"),
-    "w": ("sbuf", [M, 9 * M], "bfloat16"),
+    "w": ("sbuf", [M, 10 * M], "bfloat16"),
     "at1": ("sbuf", [M, M], "bfloat16"),
     "cd": ("sbuf", [M, 2 * B], "bfloat16"),
     "loc": ("sbuf", [M, 2 * B], "float32"),
-    "rel": ("sbuf", [M, B], "bfloat16"),
+    "hs": ("sbuf", [M, B], "bfloat16"),
+    "rel": ("sbuf", [M, H], "bfloat16"),
     "px": ("sbuf", [M, 2 * B], "bfloat16"),
-    "in1": ("sbuf", [M, 4 * H], "bfloat16"),
+    "in1": ("sbuf", [M, 2 * H], "bfloat16"),
     "in2": ("sbuf", [M, 2 * B], "bfloat16"),
     "yo": ("sbuf", [M, 2 * B], "bfloat16"),
     "pf": ("psum", [M, 512], "float32"),
@@ -27,16 +28,17 @@ SCRATCH = {
     "py1": ("psum", [M, 512], "float32"),
 }
 NLOCAL = 32
-SEMAPHORES = (["hp", "h2A0", "h2A1", "h2B", "sent"] + ["h1_%d" % i for i in range(4)] + ["q%d" % i for i in range(NLOCAL)])
+SEMAPHORES = (["hp", "h2A0", "h2A1", "h2B", "sent"] + ["h1_%d" % i for i in range(2)] + ["q%d" % i for i in range(NLOCAL)])
 
-SEND1 = {0: ((2, 3), 0), 1: ((2, 3), 1), 2: ((4, 5), 3), 3: ((4, 5), 2)}
-RSLOT = {"R0": 0, "R1": 1, "R4": 2, "R5": 3}
-SENDB = {0: (6, 3), 1: (7, 2)}
-REL = {0: ("P1", [("f", 2), ("P0", 1)]), 1: ("f", [("P0", 3), ("P1", 2)])}
-RELF = {2: ("P1", [("f", 2), ("P0", 1), ("R0", 6), ("R1", 4)]), 3: ("f", [("P0", 3), ("P1", 2), ("R0", 6), ("R1", 4)])}
-RELS = {2: ("b", [("P1", 3), ("P0", 2), ("R5", 6), ("R4", 4)]), 3: ("P0", [("b", 2), ("P1", 1), ("R5", 6), ("R4", 4)])}
-FIN = {0: [("P1", 3, 2), ("P0", 2, 1), ("B", 12, 11), ("A", 4, 3)],
-       1: [("P0", 2, 3), ("P1", 1, 2), ("B", 10, 9), ("A", 2, 1)],
+SEND1 = {0: ((2, 3), 0), 1: ((2, 3), 1), 2: ((0, 1), 0), 3: ((0, 1), 1)}
+RSLOT = {"R0": 0, "R1": 1, "R2": 0, "R3": 1}
+SEND2 = {0: (6, 7), 1: (6, 7), 2: (4, 5), 3: (4, 5)}
+HSUM = {0: ("P1", [("f", 2), ("P0", 1)]), 1: ("f", [("P0", 3), ("P1", 2)]),
+        2: ("b", [("P1", 3), ("P0", 2)]), 3: ("P0", [("b", 2), ("P1", 1)])}
+RELF = {0: ("R3", [("f", 6), ("P0", 5), ("P1", 4), ("R2", 2)]), 1: ("R3", [("f", 4), ("P0", 7), ("P1", 6), ("R2", 2)]),
+        2: ("P1", [("f", 2), ("P0", 1), ("R0", 6), ("R1", 4)]), 3: ("f", [("P0", 3), ("P1", 2), ("R0", 6), ("R1", 4)])}
+FIN = {0: [("P1", 3, 2), ("P0", 2, 1), ("B", 4, 3), ("A", 8, 7)],
+       1: [("P0", 2, 3), ("P1", 1, 2), ("B", 2, 1), ("A", 6, 5)],
        2: [("P1", 3, 2), ("P0", 2, 1), ("B", 1, 2), ("A", 4, 3)],
        3: [("P0", 2, 3), ("P1", 1, 2), ("B", 3, 4), ("A", 2, 1)]}
 
@@ -93,15 +95,11 @@ def rank_program(g, core, T, topo):
     FWD, BWD = blk(T.cd, 0), blk(T.cd, 1)
     fellow = [c for c in T.cores if c != core and same_chip(c, core)][0]
     own = {"f": (T.cd, 0), "b": (T.cd, 1), "P0": (T.px, b0), "P1": (T.px, b1)}
-    end_host = rho < 2
     my_half = half_of(core)
-    slot = {1: A1, 2: A2, 3: A3, 4: A4}
-    if end_host:
-        low = {0: 3, 1: 1}[rho]
-        hi = slot[low]
-        slot.update({8 + low: S7, 9 + low: S8})
-    else:
-        slot.update({5: S6, 6: S7})
+    slot = {1: A1, 2: A2, 3: A3, 4: A4, 5: A5, 6: A6, 7: A7, 8: A8}
+    top = max([p for k, p in RELF[rho][1]] + [max(p0, p1) for k, p0, p1 in FIN[rho]])
+    n_away = len(engines(core, peer(SEND2[rho][0])))
+    n_half = n_away // 2
 
     ld_x, ld_a, ld_at = sem(), sem(), sem()
     sy.dma_start(T.xs[:], T.x[:]).then_inc(ld_x, 16)
@@ -155,32 +153,23 @@ def rank_program(g, core, T, topo):
         else:
             q.wait_ge(T.sem["h1_%d" % RSLOT[k]], n_half)
 
-    n_away = len([e for c in T.cores if not same_chip(core, c) and topo.may_write(core, c)
-                  for e in engines(core, c)][:len(engines(core, [c for c in T.cores if not same_chip(core, c)
-                                                                  and topo.may_write(core, c)][0]))])
-    n_half = n_away // 2
+    def sum_mm(spec, bank, half):
+        plain, terms = spec
+        ms = sem()
+        width = B if half is None else H
+        for i, (k, p) in enumerate(terms):
+            ready(te, k)
+            te.matmul(bank[:, 0:width], W(slot[p]), src_of(k, half), i == 0, i == len(terms) - 1).then_inc(ms, 1)
+        return ms
 
-    v_r = sem()
-    if end_host:
-        sums = [(REL[rho], T.pr, None, T.rel[:], sem())]
-    else:
-        sums = [(RELF[rho], T.pr, my_half, blk(T.rel, 0, H), sem()), (RELS[rho], T.ps, my_half, blk(T.rel, 1, H), sem())]
-
-    def relay_mm():
-        depth = len(sums[0][0][1])
-        for i in range(depth):
-            for (plain, terms), bank, half, out, ms in sums:
-                k, p = terms[i]
-                ready(te, k)
-                width = B if half is None else H
-                te.matmul(bank[:, 0:width], W(slot[p]), src_of(k, half), i == 0, i == depth - 1).then_inc(ms, 1)
-
-    def relay_out():
-        for (plain, terms), bank, half, out, ms in sums:
-            ready(ve, plain)
-            ve.wait_ge(ms, len(terms))
-            width = B if half is None else H
-            ve.tensor_tensor(out, bank[:, 0:width], src_of(plain, half), AluOpType.add).then_inc(v_r, 1)
+    def sum_out(spec, bank, half, out, ms):
+        plain, terms = spec
+        vs = sem()
+        width = B if half is None else H
+        ready(ve, plain)
+        ve.wait_ge(ms, len(terms))
+        ve.tensor_tensor(out, bank[:, 0:width], src_of(plain, half), AluOpType.add).then_inc(vs, 1)
+        return vs
 
     carry_f()
     s1 = step(A2, [(T.at1[:], W(A1), 1), (W(A1), T.at1[:], 1)], [(ld_at, 16)])
@@ -188,21 +177,16 @@ def rank_program(g, core, T, topo):
     carry_b()
     s2 = step(A3, [(W(AT2), W(A1, 2), 2), (W(A2), W(AT2), 1)], [(c1, 1)])
     c2 = step_out(s2)
-    if end_host:
-        te.wait_ge(c2, 1)
-        relay_mm()
-        relay_out()
-        s3 = step(S6, [(W(A4), W(AT4), 1)], [(c2, 1)])
-        c3 = step_out(s3)
-        s4 = step(S7, [(W(S6), W(hi, 2), 2)], [(c3, 1)])
-        c_last = step_out(s4)
-    else:
-        s3 = step(S6, [(W(AT4), W(A1, 2), 2)], [(c2, 1)])
-        c_last = step_out(s3)
-        te.wait_ge(c_last, 1)
-        relay_mm()
-        relay_out()
+    lift = [(W(AT4), W(A1, 2), 2)]
+    if top > 6:
+        lift.append((W(AT4), W(A3, 2), 2))
+    s3 = step(A5, lift, [(c2, 1)])
+    c_last = step_out(s3)
     te.wait_ge(c_last, 1)
+    m_h = sum_mm(HSUM[rho], T.pr, None)
+    v_h = sum_out(HSUM[rho], T.pr, None, T.hs[:], m_h)
+    m_r = sum_mm(RELF[rho], T.ps, my_half)
+    v_r = sum_out(RELF[rho], T.ps, my_half, T.rel[:], m_r)
 
     v_l = sem()
     ve.wait_ge(v_f, 1)
@@ -214,8 +198,8 @@ def rank_program(g, core, T, topo):
     fin = FIN[rho]
     for i, (k, p0, p1) in enumerate(fin):
         if k == "A":
-            te.wait_ge(T.sem.h2A0, n_half)
-            te.wait_ge(T.sem.h2A1, n_half)
+            te.wait_ge(T.sem.h2A0, n_away)
+            te.wait_ge(T.sem.h2A1, n_away)
             src = blk(T.in2, 0)
         elif k == "B":
             te.wait_ge(T.sem.h2B, n_away)
@@ -265,18 +249,18 @@ def rank_program(g, core, T, topo):
         sent += len(es)
     g.remote_dma_fused(trs, local_sem=T.sem.sent)
 
-    g.wait_ge(v_r, len(sums))
-    if end_host:
-        ds = [peer(k) for k in SENDB[rho]]
-        es = engines(core, ds[0])
-        trs = [transfer(T.rel[:], blk(T.in2, 1), ds, es, T.sem.h2B)]
-        sent += len(es)
-    else:
-        trs = []
-        for j, ks in enumerate(((4, 5), (0, 1))):
-            ds = [peer(k) for k in ks]
-            es = engines(core, ds[0])[j::2]
-            trs.append(transfer(blk(T.rel, j, H), blk(T.in2, my_half, H), ds, es, T.sem["h2A%d" % my_half]))
-            sent += len(es)
-    g.remote_dma_fused(trs, local_sem=T.sem.sent)
+    d = [peer(k) for k in relays if topo.die(peer(k)) == topo.die(core)][0]
+    g.wait_ge(v_h, 1)
+    rid, pid = topo.addr(d, core)
+    es = engines(core, d)
+    g.remote_dma(out_ap=blk(T.in2, 1), in_ap=T.hs[:], remote_sem=T.sem.h2B, local_sem=T.sem.sent, pid=pid,
+                 routing_id=rid, dma_engine_mask=_pack(es))
+    sent += len(es)
+
+    g.wait_ge(v_r, 1)
+    ds = [peer(k) for k in SEND2[rho]]
+    es = engines(core, ds[0])
+    g.remote_dma_fused([transfer(T.rel[:], blk(T.in2, my_half, H), ds, es, T.sem["h2A%d" % my_half])],
+                       local_sem=T.sem.sent)
+    sent += len(es)
     g.wait_ge(T.sem.sent, sent)

from concourse.bass import DstId, RemoteDMATransfer
from concourse.mybir import AluOpType

B = 256
M = 128
H = B // 2

A1, A2, AT2, A3, A4, AT4, A5, A6, A7, A8 = range(10)

SCRATCH = {
    "xs": ("sbuf", [M, 2 * B], "bfloat16"),
    "w": ("sbuf", [M, 10 * M], "bfloat16"),
    "at1": ("sbuf", [M, M], "bfloat16"),
    "cd": ("sbuf", [M, 2 * B], "bfloat16"),
    "loc": ("sbuf", [M, 2 * B], "float32"),
    "hs": ("sbuf", [M, B], "bfloat16"),
    "rel": ("sbuf", [M, H], "bfloat16"),
    "px": ("sbuf", [M, 2 * B], "bfloat16"),
    "in1": ("sbuf", [M, 2 * H], "bfloat16"),
    "in2": ("sbuf", [M, 2 * B], "bfloat16"),
    "yo": ("sbuf", [M, 2 * B], "bfloat16"),
    "pf": ("psum", [M, 512], "float32"),
    "pb": ("psum", [M, 512], "float32"),
    "pp": ("psum", [M, 512], "float32"),
    "pr": ("psum", [M, 512], "float32"),
    "ps": ("psum", [M, 512], "float32"),
    "py0": ("psum", [M, 512], "float32"),
    "py1": ("psum", [M, 512], "float32"),
}
NLOCAL = 32
SEMAPHORES = (["hp", "h2A0", "h2A1", "h2B", "sent"] + ["h1_%d" % i for i in range(2)] + ["q%d" % i for i in range(NLOCAL)])

SEND1 = {0: ((2, 3), 0), 1: ((2, 3), 1), 2: ((0, 1), 0), 3: ((0, 1), 1)}
RSLOT = {"R0": 0, "R1": 1, "R2": 0, "R3": 1}
SEND2 = {0: (6, 7), 1: (6, 7), 2: (4, 5), 3: (4, 5)}
HSUM = {0: ("P1", [("f", 2), ("P0", 1)]), 1: ("f", [("P0", 3), ("P1", 2)]),
        2: ("b", [("P1", 3), ("P0", 2)]), 3: ("P0", [("b", 2), ("P1", 1)])}
RELF = {0: ("R3", [("f", 6), ("P0", 5), ("P1", 4), ("R2", 2)]), 1: ("R3", [("f", 4), ("P0", 7), ("P1", 6), ("R2", 2)]),
        2: ("P1", [("f", 2), ("P0", 1), ("R0", 6), ("R1", 4)]), 3: ("f", [("P0", 3), ("P1", 2), ("R0", 6), ("R1", 4)])}
FIN = {0: [("P1", 3, 2), ("P0", 2, 1), ("B", 4, 3), ("A", 8, 7)],
       1: [("P0", 2, 3), ("P1", 1, 2), ("B", 2, 1), ("A", 6, 5)],
       2: [("P1", 3, 2), ("P0", 2, 1), ("B", 1, 2), ("A", 4, 3)],
       3: [("P0", 2, 3), ("P1", 1, 2), ("B", 3, 4), ("A", 2, 1)]}


def _bits(mask):
    return [e for e in range(mask.bit_length()) if (mask >> e) & 1]


def _pack(engines):
    return sum(1 << e for e in engines)


def rank_program(g, core, T, topo):
    rank = T.rank_of(core)
    if rank is None:
        return
    n = len(T.cores)
    mirrored = rank >= n // 2
    rho = n - 1 - rank if mirrored else rank

    def peer(k):
        return T.cores[n - 1 - k if mirrored else k]

    def same_chip(p, q):
        return topo.host(p) == topo.host(q) and topo.chip(p) == topo.chip(q)

    def engines(src, dst):
        if not same_chip(src, dst):
            return _bits(topo.mask(src, dst))
        away = 0
        for c in T.cores:
            if not same_chip(src, c) and topo.may_write(src, c):
                away |= topo.mask(src, c)
        return [e for e in _bits(topo.mask(src, dst)) if not (away >> e) & 1]

    def half_of(c):
        return T.rank_of(c) % 2

    te, ve, sy, sc = g.tensor, g.vector, g.sync, g.scalar
    pool = [0]

    def sem():
        pool[0] += 1
        return T.sem["q%d" % (pool[0] - 1)]

    def blk(t, j, width=B):
        return t[:, j * width:(j + 1) * width]

    def W(j, k=1):
        return T.w[:, j * M:(j + k) * M]

    b0, b1 = (1, 0) if mirrored else (0, 1)
    X0, X1 = blk(T.xs, b0), blk(T.xs, b1)
    FWD, BWD = blk(T.cd, 0), blk(T.cd, 1)
    fellow = [c for c in T.cores if c != core and same_chip(c, core)][0]
    own = {"f": (T.cd, 0), "b": (T.cd, 1), "P0": (T.px, b0), "P1": (T.px, b1)}
    my_half = half_of(core)
    slot = {1: A1, 2: A2, 3: A3, 4: A4, 5: A5, 6: A6, 7: A7, 8: A8}
    top = max([p for k, p in RELF[rho][1]] + [max(p0, p1) for k, p0, p1 in FIN[rho]])
    n_away = len(engines(core, peer(SEND2[rho][0])))
    n_half = n_away // 2

    ld_x, ld_a, ld_at = sem(), sem(), sem()
    sy.dma_start(T.xs[:], T.x[:]).then_inc(ld_x, 16)
    sc.dma_start(W(A1), T.a[:]).then_inc(ld_a, 16)
    sc.dma_start(T.at1[:], T.at[:]).then_inc(ld_at, 16)

    m_f, m_b, v_f, v_b = sem(), sem(), sem(), sem()
    te.wait_ge(ld_a, 16)
    te.wait_ge(ld_x, 16)
    te.matmul(T.pf[:, 0:B], W(A1), X0, True, True).then_inc(m_f, 1)
    te.matmul(T.pb[:, 0:B], W(A1), X1, True, True).then_inc(m_b, 1)
    ve.wait_ge(ld_x, 16)

    def carry_f():
        ve.wait_ge(m_f, 1)
        ve.tensor_tensor(FWD, T.pf[:, 0:B], X1, AluOpType.add).then_inc(v_f, 1)

    def carry_b():
        ve.wait_ge(m_b, 1)
        ve.tensor_tensor(BWD, T.pb[:, 0:B], X0, AluOpType.add).then_inc(v_b, 1)

    def step(first, products, after):
        ms, vs = sem(), sem()
        for s, c in after:
            te.wait_ge(s, c)
        at = 0
        for lhsT, rhs, k in products:
            te.matmul(T.pp[:, at * M:(at + k) * M], lhsT, rhs, True, True).then_inc(ms, 1)
            at += k
        return (ms, len(products), first, at, vs)

    def step_out(st):
        ms, cnt, first, k, vs = st
        ve.wait_ge(ms, cnt)
        ve.tensor_copy(W(first, k), T.pp[:, 0:k * M]).then_inc(vs, 1)
        return vs

    def src_of(k, half=None):
        if k in RSLOT:
            return blk(T.in1, RSLOT[k], H)
        t, j = own[k]
        return blk(t, j) if half is None else blk(t, 2 * j + half, H)

    def ready(q, k):
        if k == "f":
            q.wait_ge(v_f, 1)
        elif k == "b":
            q.wait_ge(v_b, 1)
        elif k in own:
            q.wait_ge(T.sem.hp, len(engines(fellow, core)))
        else:
            q.wait_ge(T.sem["h1_%d" % RSLOT[k]], n_half)

    def sum_mm(spec, bank, half):
        plain, terms = spec
        ms = sem()
        width = B if half is None else H
        for i, (k, p) in enumerate(terms):
            ready(te, k)
            te.matmul(bank[:, 0:width], W(slot[p]), src_of(k, half), i == 0, i == len(terms) - 1).then_inc(ms, 1)
        return ms

    def sum_out(spec, bank, half, out, ms):
        plain, terms = spec
        vs = sem()
        width = B if half is None else H
        ready(ve, plain)
        ve.wait_ge(ms, len(terms))
        ve.tensor_tensor(out, bank[:, 0:width], src_of(plain, half), AluOpType.add).then_inc(vs, 1)
        return vs

    carry_f()
    s1 = step(A2, [(T.at1[:], W(A1), 1), (W(A1), T.at1[:], 1)], [(ld_at, 16)])
    c1 = step_out(s1)
    carry_b()
    s2 = step(A3, [(W(AT2), W(A1, 2), 2), (W(A2), W(AT2), 1)], [(c1, 1)])
    c2 = step_out(s2)
    lift = [(W(AT4), W(A1, 2), 2)]
    if top > 6:
        lift.append((W(AT4), W(A3, 2), 2))
    s3 = step(A5, lift, [(c2, 1)])
    c_last = step_out(s3)
    te.wait_ge(c_last, 1)
    m_h = sum_mm(HSUM[rho], T.pr, None)
    v_h = sum_out(HSUM[rho], T.pr, None, T.hs[:], m_h)
    m_r = sum_mm(RELF[rho], T.ps, my_half)
    v_r = sum_out(RELF[rho], T.ps, my_half, T.rel[:], m_r)

    v_l = sem()
    ve.wait_ge(v_f, 1)
    ve.wait_ge(v_b, 1)
    ve.tensor_tensor(blk(T.loc, 0), X0, BWD, AluOpType.add).then_inc(v_l, 1)
    ve.tensor_tensor(blk(T.loc, 1), FWD, X1, AluOpType.add).then_inc(v_l, 1)

    m_y0, m_y1 = sem(), sem()
    fin = FIN[rho]
    for i, (k, p0, p1) in enumerate(fin):
        if k == "A":
            te.wait_ge(T.sem.h2A0, n_away)
            te.wait_ge(T.sem.h2A1, n_away)
            src = blk(T.in2, 0)
        elif k == "B":
            te.wait_ge(T.sem.h2B, n_away)
            src = blk(T.in2, 1)
        else:
            ready(te, k)
            src = src_of(k)
        te.matmul(T.py0[:, 0:B], W(slot[p0]), src, i == 0, i == len(fin) - 1).then_inc(m_y0, 1)
        te.matmul(T.py1[:, 0:B], W(slot[p1]), src, i == 0, i == len(fin) - 1).then_inc(m_y1, 1)

    v_y0, v_y1, st0, st1 = sem(), sem(), sem(), sem()
    ve.wait_ge(v_l, 2)
    ve.wait_ge(m_y0, len(fin))
    ve.tensor_tensor(blk(T.yo, b0), T.py0[:, 0:B], blk(T.loc, 0), AluOpType.add).then_inc(v_y0, 1)
    ve.wait_ge(m_y1, len(fin))
    ve.tensor_tensor(blk(T.yo, b1), T.py1[:, 0:B], blk(T.loc, 1), AluOpType.add).then_inc(v_y1, 1)
    sy.wait_ge(v_y0, 1)
    sy.dma_start(blk(T.y, b0), blk(T.yo, b0)).then_inc(st0, 16)
    sy.wait_ge(st0, 16)
    sc.wait_ge(v_y1, 1)
    sc.dma_start(blk(T.y, b1), blk(T.yo, b1)).then_inc(st1, 16)
    sc.wait_ge(st1, 16)

    sent = 0

    def dst_id(d):
        rid, pid = topo.addr(d, core)
        return DstId(rid=rid, pnc=pid)

    def transfer(src, dst, ds, es, remote_sem):
        return RemoteDMATransfer(dst_ids=[dst_id(d) for d in ds], dma_engine_mask=_pack(es), remote_sem=remote_sem,
                                 srcs=[src], dsts=[dst for d in ds])

    g.wait_ge(ld_x, 16)
    rid, pid = topo.addr(fellow, core)
    es = engines(core, fellow)
    g.remote_dma(out_ap=T.px[:], in_ap=T.xs[:], remote_sem=T.sem.hp, local_sem=T.sem.sent, pid=pid, routing_id=rid,
                 dma_engine_mask=_pack(es))
    sent += len(es)
    relays, land = SEND1[rho]
    g.wait_ge(v_f, 1)
    trs = []
    for j, k in enumerate(relays):
        d = peer(k)
        es = engines(core, d)[j::2]
        trs.append(transfer(blk(T.cd, half_of(d), H), blk(T.in1, land, H), [d], es, T.sem["h1_%d" % land]))
        sent += len(es)
    g.remote_dma_fused(trs, local_sem=T.sem.sent)

    d = [peer(k) for k in relays if topo.die(peer(k)) == topo.die(core)][0]
    g.wait_ge(v_h, 1)
    rid, pid = topo.addr(d, core)
    es = engines(core, d)
    g.remote_dma(out_ap=blk(T.in2, 1), in_ap=T.hs[:], remote_sem=T.sem.h2B, local_sem=T.sem.sent, pid=pid,
                 routing_id=rid, dma_engine_mask=_pack(es))
    sent += len(es)

    g.wait_ge(v_r, 1)
    ds = [peer(k) for k in SEND2[rho]]
    es = engines(core, ds[0])
    g.remote_dma_fused([transfer(T.rel[:], blk(T.in2, my_half, H), ds, es, T.sem["h2A%d" % my_half])],
                       local_sem=T.sem.sent)
    sent += len(es)
    g.wait_ge(T.sem.sent, sent)
